import numpy as np
import ml_dtypes


def mxq(x, axis, fmt="e4m3"):
    dtype, down = {"e4m3": (ml_dtypes.float8_e4m3fn, 7), "e5m2": (ml_dtypes.float8_e5m2, 14)}[fmt]
    v = np.moveaxis(np.asarray(x, np.float32).astype(ml_dtypes.bfloat16).astype(np.float64), axis, -1)
    blocks = v.reshape(v.shape[:-1] + (-1, 32))
    amax = np.abs(blocks).max(-1, keepdims=True)
    byte = np.maximum(np.where(amax > 0, np.frexp(amax)[1] - 1 + 127, 0) - down, 1)
    scale = np.exp2(byte - 127.0)
    codes = (blocks / scale).astype(np.float32).astype(dtype).astype(np.float64)
    return np.moveaxis((codes * scale).reshape(v.shape), -1, axis)


WIDE = False


def mx_kscale(k):
    if not WIDE:
        return np.ones(k)
    levels = np.array([10, -10, 5, -5, 0])
    if k % 512:
        return np.exp2(np.random.permutation(np.resize(levels, k // 32))).repeat(32)
    a = np.empty((k // 512, 16))
    for p in range(k // 512):
        a[p, :8] = np.random.permutation(np.resize(levels, 8))
        for g in range(8):
            far = levels[np.abs(levels - a[p, g]) >= 10]
            a[p, g + 8] = far[np.random.randint(len(far))]
    return np.exp2(a.ravel()).repeat(32)


def f64(x):
    return np.asarray(x).astype(np.float64)


def striped(idx):
    return np.tile(idx.reshape(-1, 16).T, (8, 1)).astype(np.uint16)


def unstriped(offs):
    return offs[:16].T.reshape(-1).astype(np.int64)


def pack_weight(w):
    k, n = w.shape
    w = f64(np.asarray(w, np.float32).astype(ml_dtypes.bfloat16)).reshape(k // 32, 32, n)
    amax = np.abs(w).max(1)
    byte = np.clip(np.where(amax > 0, np.frexp(amax)[1] - 1 + 127 - 7, 1), 1, 254)
    scaled = (w * np.exp2(127.0 - byte)[:, None, :]).reshape(k, n).astype(np.float32)
    words = np.ascontiguousarray(scaled.reshape(k // 512, 128, 4, n).transpose(0, 1, 3, 2)).astype(ml_dtypes.float8_e4m3fn).view(np.uint8)
    return words, np.ascontiguousarray(byte.astype(np.uint8).reshape(k // 512, 16, n))


def unpack_weight(words, scales):
    g, p, n, _ = words.shape
    vals = np.ascontiguousarray(words).view(ml_dtypes.float8_e4m3fn).astype(np.float64) * np.repeat(np.exp2(scales.astype(np.float64) - 127.0), 8, axis=1)[..., None]
    return vals.transpose(0, 1, 3, 2).reshape(g * 512, n)


E2M1 = np.array([0.0, 0.5, 1.0, 1.5, 2.0, 3.0, 4.0, 6.0, -0.0, -0.5, -1.0, -1.5, -2.0, -3.0, -4.0, -6.0])


def pack_fp4(w):
    k, n = w.shape
    w = f64(np.asarray(w, np.float32).astype(ml_dtypes.bfloat16)).reshape(k // 32, 32, n)
    amax = np.abs(w).max(1)
    mant, ex = np.frexp(amax / 6.0)
    byte = np.clip(np.where(amax > 0, np.where(mant > 0.5, ex, ex - 1) + 127, 1), 1, 254)
    scaled = (w * np.exp2(127.0 - byte)[:, None, :]).reshape(k, n).astype(np.float32)
    c = np.ascontiguousarray(scaled.reshape(k // 512, 128, 4, n).transpose(0, 1, 3, 2)).astype(ml_dtypes.float4_e2m1fn).view(np.uint8) & 0xF
    words = (c[..., 0::2] | (c[..., 1::2] << 4)).reshape(k // 512, 128, 2 * n)
    return np.ascontiguousarray(words), np.ascontiguousarray(byte.astype(np.uint8).reshape(k // 512, 16, n))


def unpack_fp4(words, scales):
    g, _, n = scales.shape
    words = np.ascontiguousarray(words).reshape(g, 128, n, 2)
    nib = np.empty((g, 128, n, 4), np.uint8)
    nib[..., 0::2] = words & 0xF
    nib[..., 1::2] = words >> 4
    vals = E2M1[nib] * np.repeat(np.exp2(scales.astype(np.float64) - 127.0), 8, axis=1)[..., None]
    return vals.transpose(0, 1, 3, 2).reshape(g * 512, n)


K, T, S, N, H, U = 512, 1024, 512, 128, 512, 1024


def setup_inputs():
    n = np.random.standard_normal
    s = mx_kscale(K)[:, None]
    u = mx_kscale(H)
    packed_xT = pack_weight(n((K, T)) * s)
    packed_w1 = pack_fp4(n((K, H)) / np.sqrt(K) / s)
    packed_w2 = pack_fp4(n((K, H)) / np.sqrt(K) / s)
    packed_w3 = pack_fp4(n((H, N)) / np.sqrt(H) / u[:, None])
    return {
        "x_words": packed_xT[0],
        "x_scales": packed_xT[1],
        "w1_words": packed_w1[0],
        "w1_scales": packed_w1[1],
        "w2_words": packed_w2[0],
        "w2_scales": packed_w2[1],
        "por": (np.random.uniform(0.08, 0.35, (H, U))).astype(np.float32),
        "rho": (np.random.uniform(0.8, 1.2, (H, U))).astype(np.float32),
        "unit": (np.random.uniform(0.6, 1.4, (H, 1)) * u[:, None]).astype(np.float32),
        "w3_words": packed_w3[0],
        "w3_scales": packed_w3[1],
        "offs": striped(np.random.permutation(T)[:S]),
        "rk": striped(np.random.permutation(np.concatenate([np.arange(S), np.random.randint(0, S, U - S)]))),
        "fl": striped(np.random.permutation(np.concatenate([np.arange(S), np.random.randint(0, S, U - S)]))),
    }


def reference(x_words, x_scales, w1_words, w1_scales, w2_words, w2_scales, por, rho, unit, w3_words, w3_scales, offs, rk, fl):
    xq = unpack_weight(x_words, x_scales)[:, unstriped(offs)]
    kd = unpack_fp4(w1_words, w1_scales).T @ xq
    kdry = np.log(np.exp(kd) + 1.0) + 0.4
    dr = kdry[:, unstriped(rk)]
    biot = -1.0 * (0.8 * (dr / (dr + 1.5))) + 1.0
    gd = unpack_fp4(w2_words, w2_scales).T @ xq
    kfl = 0.5 * (np.log(np.exp(gd) + 1.0)) + 0.1
    fr = kfl[:, unstriped(fl)]
    ksat = dr + ((biot) ** 2) / (f64(por) / fr + 0.3 * (biot - f64(por)))
    imp = np.sqrt(ksat * f64(rho))
    hid = f64(unit) * ((imp - dr) / (imp + dr))
    return unpack_fp4(w3_words, w3_scales).T @ mxq(hid, 0, "e4m3")

@@ -1,0 +1,229 @@
+from contextlib import ExitStack
+
+import concourse.mybir as mybir
+
+K, T, S, N, H, U = 512, 1024, 512, 128, 512, 1024
+FLOPS = 2 * (2 * K * H * S + H * N * U)
+
+F32 = mybir.dt.float32
+BF16 = mybir.dt.bfloat16
+I32 = mybir.dt.int32
+U32 = mybir.dt.uint32
+U16 = mybir.dt.uint16
+U8 = mybir.dt.uint8
+FP8X4 = mybir.dt.float8_e4m3fn_x4
+FP4X4 = mybir.dt.float4_e2m1fn_x4
+ALU = mybir.AluOpType
+ACT = mybir.ActivationFunctionType
+
+P = 128
+PACK = 4
+CHUNK = 256
+TINY = 1e-18
+LN_SCALE = 2.0**-16
+SHIFT_ON_VECTOR = 2
+POR_SLOT = (1, 0, 8, 10)
+RHO_SLOT = (2, 3, 9, 6)
+
+
+def load_scale_rows(queue, plane, rows):
+    for q in range(4):
+        queue.dma_start(out=plane[32 * q : 32 * q + 4, :].bitcast(I32), in_=rows[4 * q : 4 * q + 4, :].bitcast(I32))
+
+
+def tile_picked_ygassm_refl_p_kernel(
+    tc, x_words, x_scales, w1_words, w1_scales, w2_words, w2_scales, por, rho, unit, w3_words, w3_scales, offs, rk, fl, out
+):
+    nc = tc.nc
+    with ExitStack() as ctx:
+        keep = ctx.enter_context(tc.tile_pool(name="keep", bufs=1))
+        psum = ctx.enter_context(tc.psum_pool(name="psum", bufs=1))
+
+        offs_t = keep.tile([P, S // 16], U16)
+        rk_t = keep.tile([P, U // 16], U16)
+        fl_t = keep.tile([P, U // 16], U16)
+        x_w = keep.tile([P, T], U32, align_bytes=64, tag="in0")
+        x_s = keep.tile([P, T], U8, align_bytes=64, tag="in1")
+
+        xg_w = keep.tile([P, S], U32, align_bytes=64, tag="in6")
+        xg_s = keep.tile([P, S], U8, align_bytes=64, tag="in7")
+        w_deal = [keep.tile([P, 2 * H], U8, name=f"w_deal{i}", align_bytes=64, tag=f"in{8 + i}") for i in range(2)]
+        s_deal = [keep.tile([P, H], U8, name=f"s_deal{i}", align_bytes=64, tag=f"in{10 + i}") for i in range(2)]
+
+        def load_weight(words, scales):
+            w_raw = keep.tile([P, 2 * H], U8, name="w_raw", align_bytes=64, tag="in2")
+            s_raw = keep.tile([P, H], U8, name="s_raw", align_bytes=64, tag="in3")
+            nc.gpsimd.memset(s_raw[:].bitcast(I32), 0)
+            nc.sync.dma_start(out=w_raw[:].bitcast(I32), in_=words[0].bitcast(I32))
+            return w_raw, s_raw
+
+        def deal(i, w_raw, s_raw):
+            nc.vector.tensor_copy(
+                out=w_deal[i][:].rearrange("p (t m b) -> p t m b", t=PACK, b=2),
+                in_=w_raw[:].rearrange("p (m t b) -> p t m b", t=PACK, b=2),
+            )
+            nc.vector.tensor_copy(
+                out=s_deal[i][:].rearrange("p (t m) -> p t m", t=PACK),
+                in_=s_raw[:].rearrange("p (m t) -> p t m", t=PACK),
+            )
+
+        nc.vector.memset(x_s[:].bitcast(I32), 0)
+        nc.sync.dma_start(out=offs_t[:], in_=offs)
+        w_raw, s_raw = load_weight(w2_words, w2_scales)
+        nc.sync.dma_start(out=x_w[:].bitcast(I32), in_=x_words[0].rearrange("p n t -> p (n t)").bitcast(I32))
+        load_scale_rows(nc.sync, x_s, x_scales[0])
+        load_scale_rows(nc.sync, s_raw, w2_scales[0])
+        nc.sync.dma_start(out=fl_t[:], in_=fl)
+        nc.sync.dma_start(out=rk_t[:], in_=rk)
+        nc.vector.tensor_copy(out=xg_s[:], in_=x_s[:].indirect(offs_t[:]))
+        nc.vector.tensor_copy(out=xg_w[:], in_=x_w[:].indirect(offs_t[:]))
+        deal(0, w_raw, s_raw)
+        w_raw, s_raw = load_weight(w1_words, w1_scales)
+        load_scale_rows(nc.sync, s_raw, w1_scales[0])
+        deal(1, w_raw, s_raw)
+
+        banks = [[psum.tile([P, S], F32, name=f"bank{i}{t}") for t in range(PACK)] for i in range(2)]
+        tabs = [[keep.tile([P, 3 * S], F32, name=f"tab{i}{t}") for t in range(PACK)] for i in range(2)]
+        slot0, slot1, slot2 = slice(0, S), slice(S, 2 * S), slice(2 * S, 3 * S)
+
+        for i in range(2):
+            for t in range(PACK):
+                nc.tensor.matmul_mx(
+                    out=banks[i][t][:],
+                    lhsT=w_deal[i][:, 2 * P * t : 2 * P * (t + 1)].bitcast(FP4X4),
+                    lhsT_scale=s_deal[i][:, P * t : P * (t + 1)],
+                    rhs=xg_w[:].bitcast(FP8X4),
+                    rhs_scale=xg_s[:],
+                    start=True,
+                    stop=True,
+                )
+        por_t = [keep.tile([P, U], F32, name=f"por{t}", align_bytes=64, tag=f"in{POR_SLOT[t]}") for t in range(PACK)]
+        rho_t = [keep.tile([P, U], F32, name=f"rho{t}", align_bytes=64, tag=f"in{RHO_SLOT[t]}") for t in range(PACK)]
+        por_rows = por.rearrange("(p t) r -> p t r", t=PACK)
+        rho_rows = rho.rearrange("(p t) r -> p t r", t=PACK)
+        for t in range(PACK):
+            nc.sync.dma_start(out=por_t[t][:], in_=por_rows[:, t, :])
+        for t in range(PACK):
+            nc.sync.dma_start(out=rho_t[t][:], in_=rho_rows[:, t, :])
+
+        unit_t = keep.tile([P, PACK], F32, align_bytes=64, tag="in11")
+        w3_w = keep.tile([P, 2 * N], U8, align_bytes=64, tag="in7")
+        w3_s = keep.tile([P, N], U8, align_bytes=64)
+        nc.sync.dma_start(out=w3_w[:].bitcast(I32), in_=w3_words[0].bitcast(I32))
+        nc.gpsimd.memset(w3_s[:].bitcast(I32), 0)
+        nc.sync.dma_start(out=unit_t[:], in_=unit.rearrange("(p t) o -> p (t o)", t=PACK))
+        load_scale_rows(nc.sync, w3_s, w3_scales[0])
+
+        fluid, rock = tabs
+        fluid_bank, rock_bank = banks
+        for t in range(PACK):
+            nc.scalar.activation(fluid[t][:, slot2], fluid_bank[t][:], ACT.Sigmoid, scale=-1.0)
+        for t in range(PACK):
+            nc.scalar.activation(fluid[t][:, slot2], fluid[t][:, slot2], ACT.Ln, bias=TINY)
+            nc.vector.scalar_tensor_tensor(
+                fluid[t][:, slot1], fluid[t][:, slot2], -1.0, fluid_bank[t][:], ALU.mult, ALU.max
+            )
+        for t in range(PACK):
+            nc.vector.tensor_scalar(rock[t][:, slot2], rock_bank[t][:], 40.0, None, ALU.min)
+        for t in range(PACK):
+            nc.scalar.activation(fluid[t][:, slot2], fluid[t][:, slot1], ACT.Ln, scale=0.5, bias=0.1)
+        for t in range(PACK):
+            nc.scalar.activation(fluid[t][:, slot0], fluid[t][:, slot2], ACT.Exp, scale=-1.0)
+            if t < SHIFT_ON_VECTOR:
+                nc.vector.tensor_scalar(fluid[t][:, slot0], fluid[t][:, slot0], -0.3, None, ALU.add)
+            else:
+                nc.scalar.activation(fluid[t][:, slot0], fluid[t][:, slot0], ACT.Copy, bias=-0.3)
+        for t in range(PACK):
+            nc.scalar.activation(rock[t][:, slot1], rock[t][:, slot2], ACT.Exp)
+
+        big = keep.tile([P, PACK, U], F32)
+        num = keep.tile([P, PACK, U], F32)
+        den = []
+
+        def pore_term(t):
+            den.append(keep.tile([P, U], F32, name=f"den{t}"))
+            nc.vector.tensor_tensor(den[t][:], fluid[t][:].indirect(fl_t[:]), por_t[t][:], ALU.mult)
+
+        def rock_table(t, tag):
+            soft = keep.tile([P, S], F32, name=f"soft{t}", tag=tag)
+            nc.scalar.activation(soft[:], rock[t][:, slot1], ACT.Ln, bias=1.0)
+            nc.vector.tensor_tensor(rock[t][:, slot0], soft[:], rock_bank[t][:], ALU.max)
+
+        for t in range(PACK - 1):
+            pore_term(t)
+        rock_table(0, "soft0")
+        rock_table(1, "den3")
+        pore_term(3)
+        rock_table(2, "soft2")
+        rock_table(3, "soft3")
+
+        def fetch(t):
+            nc.scalar.activation(big[:, t, :], rock[t][:].indirect(rk_t[:]), ACT.Copy, bias=1.9)
+            nc.scalar.activation(num[:, t, :], big[:, t, :], ACT.Square, scale=0.2, bias=1.2)
+
+        def step(t, k):
+            if k == 0:
+                nc.vector.scalar_tensor_tensor(den[t][:], den[t][:], 0.06, big[:, t, :], ALU.add, ALU.mult)
+            if k == 1:
+                nc.vector.scalar_tensor_tensor(den[t][:], den[t][:], 0.36, big[:, t, :], ALU.add, ALU.mult)
+            if k == 2:
+                nc.vector.scalar_tensor_tensor(por_t[t][:], big[:, t, :], -1.5, den[t][:], ALU.add, ALU.mult)
+                nc.scalar.activation(big[:, t, :], por_t[t][:], ACT.Square)
+                nc.scalar.activation(big[:, t, :], big[:, t, :], ACT.Ln, scale=LN_SCALE)
+            if k == 3:
+                nc.vector.tensor_tensor(den[t][:], den[t][:], rho_t[t][:], ALU.mult)
+            if k == 4:
+                nc.vector.tensor_tensor(num[:, t, :], num[:, t, :], por_t[t][:], ALU.add)
+            if k == 5:
+                parts = 2 if t == PACK - 1 else 1
+                for h in range(parts):
+                    cols = slice(h * U // parts, (h + 1) * U // parts)
+                    nc.vector.tensor_tensor(num[:, t, cols], num[:, t, cols], den[t][:, cols], ALU.mult)
+                    nc.scalar.activation(num[:, t, cols], num[:, t, cols], ACT.Ln, scale=LN_SCALE)
+
+        for t in range(PACK):
+            fetch(t)
+        for t in range(PACK):
+            for k in range(6):
+                step(t, k)
+
+        chunks = U // CHUNK
+        refl = [keep.tile([P, CHUNK, PACK], F32, name=f"refl{c}") for c in range(chunks)]
+        hid = [keep.tile([P, CHUNK, PACK], BF16, name=f"hid{c}", align_bytes=64) for c in range(chunks)]
+        hq_w = [keep.tile([P, CHUNK], U32, name=f"hq_w{c}", align_bytes=64) for c in range(chunks)]
+        hq_s = [keep.tile([P, CHUNK], U8, name=f"hq_s{c}", align_bytes=64) for c in range(chunks)]
+        res = [keep.tile([P, CHUNK], F32, name=f"res{c}") for c in range(chunks)]
+
+        def weigh(c):
+            cols = slice(c * CHUNK, (c + 1) * CHUNK)
+            nc.scalar.activation(refl[c][:], num[:, :, cols].rearrange("p t c -> p c t"), ACT.Tanh, scale=0.25)
+            nc.vector.tensor_tensor(
+                hid[c][:], refl[c][:], unit_t[:].unsqueeze(1).to_broadcast([P, CHUNK, PACK]), ALU.mult
+            )
+
+        def finish(c):
+            cols = slice(c * CHUNK, (c + 1) * CHUNK)
+            nc.vector.quantize_mx(
+                out=hq_w[c][:].bitcast(FP8X4), scales=hq_s[c][:], in_=hid[c][:].rearrange("p c t -> p (c t)")
+            )
+            acc = psum.tile([P, S], F32, name=f"bank0{c}")
+            nc.tensor.matmul_mx(
+                out=acc[:, 0:CHUNK],
+                lhsT=w3_w[:].bitcast(FP4X4),
+                lhsT_scale=w3_s[:],
+                rhs=hq_w[c][:].bitcast(FP8X4),
+                rhs_scale=hq_s[c][:],
+                start=True,
+                stop=True,
+            )
+            nc.scalar.copy(res[c][:], acc[:, 0:CHUNK])
+            nc.sync.dma_start(out=out[:, cols], in_=res[c][:])
+
+        for c in range(chunks):
+            cols = slice(c * CHUNK, (c + 1) * CHUNK)
+            nc.vector.tensor_tensor(num[:, :, cols], num[:, :, cols], big[:, :, cols], ALU.subtract)
+        weigh(0)
+        for c in range(1, chunks):
+            weigh(c)
+            finish(c - 1)
+        finish(chunks - 1)

@@ -19,15 +19,17 @@ ACT = mybir.ActivationFunctionType
 P = 128
 PACK = 4
 CHUNK = 256
+HALF = S // 2
+WIDTHS = (256, 256, 256, 128, 128)
 TINY = 1e-18
 LN_SCALE = 2.0**-16
-SHIFT_ON_VECTOR = 2
-POR_SLOT = (1, 0, 8, 10)
-RHO_SLOT = (2, 3, 9, 6)
+SHIFT_ON_VECTOR = 3
+POR_SLOT = (2, 0, 8, 10)
+RHO_SLOT = (1, 9, 6, 12)
 
 
-def load_scale_rows(queue, plane, rows):
-    for q in range(4):
+def load_scale_rows(queue, plane, rows, quadrants=range(4)):
+    for q in quadrants:
         queue.dma_start(out=plane[32 * q : 32 * q + 4, :].bitcast(I32), in_=rows[4 * q : 4 * q + 4, :].bitcast(I32))
 
 
@@ -45,185 +47,251 @@ def tile_picked_ygassm_refl_p_kernel(
         x_w = keep.tile([P, T], U32, align_bytes=64, tag="in0")
         x_s = keep.tile([P, T], U8, align_bytes=64, tag="in1")
 
-        xg_w = keep.tile([P, S], U32, align_bytes=64, tag="in6")
-        xg_s = keep.tile([P, S], U8, align_bytes=64, tag="in7")
-        w_deal = [keep.tile([P, 2 * H], U8, name=f"w_deal{i}", align_bytes=64, tag=f"in{8 + i}") for i in range(2)]
-        s_deal = [keep.tile([P, H], U8, name=f"s_deal{i}", align_bytes=64, tag=f"in{10 + i}") for i in range(2)]
+        xg_w = []
+        xg_s = []
 
-        def load_weight(words, scales):
+        def load_words(words):
             w_raw = keep.tile([P, 2 * H], U8, name="w_raw", align_bytes=64, tag="in2")
-            s_raw = keep.tile([P, H], U8, name="s_raw", align_bytes=64, tag="in3")
-            nc.gpsimd.memset(s_raw[:].bitcast(I32), 0)
             nc.sync.dma_start(out=w_raw[:].bitcast(I32), in_=words[0].bitcast(I32))
-            return w_raw, s_raw
+            return w_raw
 
-        def deal(i, w_raw, s_raw):
+        def load_scales(scales, tag):
+            s_raw = keep.tile([P, H], U8, name="s_raw", align_bytes=64, tag=tag)
+            nc.gpsimd.memset(s_raw[:].bitcast(I32), 0)
+            load_scale_rows(nc.sync, s_raw, scales[0])
+            return s_raw
+
+        def deal_words(w_raw, tag):
+            w_deal = keep.tile([P, 2 * H], U8, name="w_deal", align_bytes=64, tag=tag)
             nc.vector.tensor_copy(
-                out=w_deal[i][:].rearrange("p (t m b) -> p t m b", t=PACK, b=2),
+                out=w_deal[:].rearrange("p (t m b) -> p t m b", t=PACK, b=2),
                 in_=w_raw[:].rearrange("p (m t b) -> p t m b", t=PACK, b=2),
             )
+            return w_deal
+
+        def deal_scales(s_raw, tag):
+            s_deal = keep.tile([P, H], U8, name="s_deal", align_bytes=64, tag=tag)
             nc.vector.tensor_copy(
-                out=s_deal[i][:].rearrange("p (t m) -> p t m", t=PACK),
+                out=s_deal[:].rearrange("p (t m) -> p t m", t=PACK),
                 in_=s_raw[:].rearrange("p (m t) -> p t m", t=PACK),
             )
+            return s_deal
+
+        def product(acc, w_deal, s_deal, t, h):
+            nc.tensor.matmul_mx(
+                out=acc,
+                lhsT=w_deal[:, 2 * P * t : 2 * P * (t + 1)].bitcast(FP4X4),
+                lhsT_scale=s_deal[:, P * t : P * (t + 1)],
+                rhs=xg_w[h][:].bitcast(FP8X4),
+                rhs_scale=xg_s[h][:],
+                start=True,
+                stop=True,
+            )
+
+        def pick(h, word_tag, scale_tag):
+            entries = offs_t[:, h * HALF // 16 : (h + 1) * HALF // 16]
+            xg_w.append(keep.tile([P, HALF], U32, name="xg_w", align_bytes=64, tag=word_tag))
+            xg_s.append(keep.tile([P, HALF], U8, name="xg_s", align_bytes=64, tag=scale_tag))
+            nc.vector.tensor_copy(out=xg_w[h][:], in_=x_w[:].indirect(entries))
+            nc.vector.tensor_copy(out=xg_s[h][:], in_=x_s[:].indirect(entries))
+
+        def load_planes(src, name, slots):
+            rows = src.rearrange("(p t) r -> p t r", t=PACK)
+            tiles = [keep.tile([P, U], F32, name=f"{name}{t}", align_bytes=64, tag=f"in{slots[t]}") for t in range(PACK)]
+            for t in range(PACK):
+                nc.sync.dma_start(out=tiles[t][:], in_=rows[:, t, :])
+            return tiles
 
         nc.vector.memset(x_s[:].bitcast(I32), 0)
         nc.sync.dma_start(out=offs_t[:], in_=offs)
-        w_raw, s_raw = load_weight(w2_words, w2_scales)
-        nc.sync.dma_start(out=x_w[:].bitcast(I32), in_=x_words[0].rearrange("p n t -> p (n t)").bitcast(I32))
-        load_scale_rows(nc.sync, x_s, x_scales[0])
-        load_scale_rows(nc.sync, s_raw, w2_scales[0])
         nc.sync.dma_start(out=fl_t[:], in_=fl)
         nc.sync.dma_start(out=rk_t[:], in_=rk)
-        nc.vector.tensor_copy(out=xg_s[:], in_=x_s[:].indirect(offs_t[:]))
-        nc.vector.tensor_copy(out=xg_w[:], in_=x_w[:].indirect(offs_t[:]))
-        deal(0, w_raw, s_raw)
-        w_raw, s_raw = load_weight(w1_words, w1_scales)
-        load_scale_rows(nc.sync, s_raw, w1_scales[0])
-        deal(1, w_raw, s_raw)
-
-        banks = [[psum.tile([P, S], F32, name=f"bank{i}{t}") for t in range(PACK)] for i in range(2)]
-        tabs = [[keep.tile([P, 3 * S], F32, name=f"tab{i}{t}") for t in range(PACK)] for i in range(2)]
-        slot0, slot1, slot2 = slice(0, S), slice(S, 2 * S), slice(2 * S, 3 * S)
-
-        for i in range(2):
+        w2_raw = load_words(w2_words)
+        load_scale_rows(nc.sync, x_s, x_scales[0], range(0, 1))
+        nc.sync.dma_start(out=x_w[:].bitcast(I32), in_=x_words[0].rearrange("p n t -> p (n t)").bitcast(I32))
+        load_scale_rows(nc.sync, x_s, x_scales[0], range(1, 4))
+        s2_raw = load_scales(w2_scales, "in3")
+        w2_deal = deal_words(w2_raw, "in8")
+        pick(0, "in6", "in7")
+        s2_deal = deal_scales(s2_raw, "in10")
+        pick(1, "in12", "in3")
+        fluid_bank = [psum.tile([P, S], F32, name=f"bank0{b}") for b in range(PACK)]
+        for h in range(2):
             for t in range(PACK):
-                nc.tensor.matmul_mx(
-                    out=banks[i][t][:],
-                    lhsT=w_deal[i][:, 2 * P * t : 2 * P * (t + 1)].bitcast(FP4X4),
-                    lhsT_scale=s_deal[i][:, P * t : P * (t + 1)],
-                    rhs=xg_w[:].bitcast(FP8X4),
-                    rhs_scale=xg_s[:],
-                    start=True,
-                    stop=True,
-                )
-        por_t = [keep.tile([P, U], F32, name=f"por{t}", align_bytes=64, tag=f"in{POR_SLOT[t]}") for t in range(PACK)]
-        rho_t = [keep.tile([P, U], F32, name=f"rho{t}", align_bytes=64, tag=f"in{RHO_SLOT[t]}") for t in range(PACK)]
-        por_rows = por.rearrange("(p t) r -> p t r", t=PACK)
-        rho_rows = rho.rearrange("(p t) r -> p t r", t=PACK)
-        for t in range(PACK):
-            nc.sync.dma_start(out=por_t[t][:], in_=por_rows[:, t, :])
-        for t in range(PACK):
-            nc.sync.dma_start(out=rho_t[t][:], in_=rho_rows[:, t, :])
+                acc = fluid_bank[2 * h + t // 2][:, (t % 2) * HALF : (t % 2 + 1) * HALF]
+                product(acc, w2_deal, s2_deal, t, h)
+        w1_deal = deal_words(load_words(w1_words), "in9")
+        s1_raw = load_scales(w1_scales, "in1")
 
-        unit_t = keep.tile([P, PACK], F32, align_bytes=64, tag="in11")
+        unit_t = keep.tile([P, PACK], F32, align_bytes=64, tag="in0")
+        nc.sync.dma_start(out=unit_t[:], in_=unit.rearrange("(p t) o -> p (t o)", t=PACK))
+        unit_rep = keep.tile([P, CHUNK, PACK], F32)
+        nc.vector.tensor_copy(out=unit_rep[:], in_=unit_t[:].unsqueeze(1).to_broadcast([P, CHUNK, PACK]))
+        por_t = load_planes(por, "por", POR_SLOT)
+
+        fluid = [keep.tile([P, 3 * S], F32, name=f"fluid{t}") for t in range(PACK)]
+        rock = [keep.tile([P, 3 * S], F32, name=f"rock{t}") for t in range(PACK)]
+        slot0, slot1, slot2 = slice(0, S), slice(S, 2 * S), slice(2 * S, 3 * S)
+        last = keep.tile([P, S], F32, align_bytes=64, tag="in11")
+        sig = [last[:] if b == 1 else fluid[b][:, slot2] for b in range(PACK)]
+        plus_f = keep.tile([P, 2, PACK, HALF], F32)
+        for b in range(PACK):
+            nc.scalar.activation(sig[b], fluid_bank[b][:], ACT.Sigmoid, scale=-1.0)
+        for b in (0, 2, 1, 3):
+            nc.scalar.activation(sig[b], sig[b], ACT.Ln, bias=TINY)
+            both = plus_f[:, b // 2, 2 * (b % 2) : 2 * (b % 2) + 2, :].rearrange("p t c -> p (t c)")
+            nc.vector.scalar_tensor_tensor(both, sig[b], -1.0, fluid_bank[b][:], ALU.mult, ALU.max)
+        s1_deal = deal_scales(s1_raw, "in11")
+        rock_bank = [psum.tile([P, S], F32, name=f"bank1{t}") for t in range(PACK)]
+        for t in range(PACK):
+            for h in range(2):
+                product(rock_bank[t][:, h * HALF : (h + 1) * HALF], w1_deal, s1_deal, t, h)
+        for t in range(PACK):
+            nc.vector.tensor_scalar(rock[t][:, slot2], rock_bank[t][:], 40.0, None, ALU.min)
+
+        rho_t = load_planes(rho, "rho", RHO_SLOT)
         w3_w = keep.tile([P, 2 * N], U8, align_bytes=64, tag="in7")
         w3_s = keep.tile([P, N], U8, align_bytes=64)
         nc.sync.dma_start(out=w3_w[:].bitcast(I32), in_=w3_words[0].bitcast(I32))
         nc.gpsimd.memset(w3_s[:].bitcast(I32), 0)
-        nc.sync.dma_start(out=unit_t[:], in_=unit.rearrange("(p t) o -> p (t o)", t=PACK))
         load_scale_rows(nc.sync, w3_s, w3_scales[0])
 
-        fluid, rock = tabs
-        fluid_bank, rock_bank = banks
         for t in range(PACK):
-            nc.scalar.activation(fluid[t][:, slot2], fluid_bank[t][:], ACT.Sigmoid, scale=-1.0)
+            both = fluid[t][:, slot1].rearrange("p (h c) -> p h c", h=2)
+            nc.scalar.activation(both, plus_f[:, :, t, :], ACT.Ln, scale=0.5, bias=0.1)
         for t in range(PACK):
-            nc.scalar.activation(fluid[t][:, slot2], fluid[t][:, slot2], ACT.Ln, bias=TINY)
-            nc.vector.scalar_tensor_tensor(
-                fluid[t][:, slot1], fluid[t][:, slot2], -1.0, fluid_bank[t][:], ALU.mult, ALU.max
-            )
-        for t in range(PACK):
-            nc.vector.tensor_scalar(rock[t][:, slot2], rock_bank[t][:], 40.0, None, ALU.min)
-        for t in range(PACK):
-            nc.scalar.activation(fluid[t][:, slot2], fluid[t][:, slot1], ACT.Ln, scale=0.5, bias=0.1)
-        for t in range(PACK):
-            nc.scalar.activation(fluid[t][:, slot0], fluid[t][:, slot2], ACT.Exp, scale=-1.0)
-            if t < SHIFT_ON_VECTOR:
-                nc.vector.tensor_scalar(fluid[t][:, slot0], fluid[t][:, slot0], -0.3, None, ALU.add)
-            else:
-                nc.scalar.activation(fluid[t][:, slot0], fluid[t][:, slot0], ACT.Copy, bias=-0.3)
+            nc.scalar.activation(fluid[t][:, slot0 if t == PACK - 1 else slot2], fluid[t][:, slot1], ACT.Exp, scale=-1.0)
         for t in range(PACK):
             nc.scalar.activation(rock[t][:, slot1], rock[t][:, slot2], ACT.Exp)
+        soft = [keep.tile([P, S], F32, name=f"soft{t}") for t in range(PACK)]
+        for t in range(PACK):
+            nc.scalar.activation(soft[t][:], rock[t][:, slot1], ACT.Ln, bias=1.0)
 
         big = keep.tile([P, PACK, U], F32)
         num = keep.tile([P, PACK, U], F32)
-        den = []
+        den = [keep.tile([P, U], F32, name=f"den{t}") for t in range(PACK - 1)]
+        whole = slice(0, U)
+        halves = (slice(0, U // 2), slice(U // 2, U))
 
-        def pore_term(t):
-            den.append(keep.tile([P, U], F32, name=f"den{t}"))
-            nc.vector.tensor_tensor(den[t][:], fluid[t][:].indirect(fl_t[:]), por_t[t][:], ALU.mult)
+        def entries(tile, cols):
+            return tile[:, cols.start // 16 : cols.stop // 16]
 
-        def rock_table(t, tag):
-            soft = keep.tile([P, S], F32, name=f"soft{t}", tag=tag)
-            nc.scalar.activation(soft[:], rock[t][:, slot1], ACT.Ln, bias=1.0)
-            nc.vector.tensor_tensor(rock[t][:, slot0], soft[:], rock_bank[t][:], ALU.max)
+        def shift(t):
+            nc.vector.tensor_scalar(fluid[t][:, slot0], fluid[t][:, slot2], -0.3, None, ALU.add)
 
-        for t in range(PACK - 1):
-            pore_term(t)
-        rock_table(0, "soft0")
-        rock_table(1, "den3")
-        pore_term(3)
-        rock_table(2, "soft2")
-        rock_table(3, "soft3")
+        def pore_term(dst, t, cols):
+            nc.vector.tensor_tensor(dst, fluid[t][:].indirect(entries(fl_t, cols)), por_t[t][:, cols], ALU.mult)
 
-        def fetch(t):
-            nc.scalar.activation(big[:, t, :], rock[t][:].indirect(rk_t[:]), ACT.Copy, bias=1.9)
+        def rock_table(t):
+            nc.vector.tensor_tensor(rock[t][:, slot0], soft[t][:], rock_bank[t][:], ALU.max)
+
+        def fetch(t, cols):
+            nc.scalar.activation(big[:, t, cols], rock[t][:].indirect(entries(rk_t, cols)), ACT.Copy, bias=1.9)
+
+        def square(t):
             nc.scalar.activation(num[:, t, :], big[:, t, :], ACT.Square, scale=0.2, bias=1.2)
 
-        def step(t, k):
+        def step(t, k, cols=whole, src=None):
             if k == 0:
-                nc.vector.scalar_tensor_tensor(den[t][:], den[t][:], 0.06, big[:, t, :], ALU.add, ALU.mult)
+                src = den[t][:, cols] if src is None else src
+                nc.vector.scalar_tensor_tensor(den[t][:, cols], src, 0.06, big[:, t, cols], ALU.add, ALU.mult)
             if k == 1:
-                nc.vector.scalar_tensor_tensor(den[t][:], den[t][:], 0.36, big[:, t, :], ALU.add, ALU.mult)
+                nc.vector.scalar_tensor_tensor(den[t][:, cols], den[t][:, cols], 0.36, big[:, t, cols], ALU.add, ALU.mult)
             if k == 2:
-                nc.vector.scalar_tensor_tensor(por_t[t][:], big[:, t, :], -1.5, den[t][:], ALU.add, ALU.mult)
-                nc.scalar.activation(big[:, t, :], por_t[t][:], ACT.Square)
-                nc.scalar.activation(big[:, t, :], big[:, t, :], ACT.Ln, scale=LN_SCALE)
+                nc.vector.scalar_tensor_tensor(por_t[t][:, cols], big[:, t, cols], -1.5, den[t][:, cols], ALU.add, ALU.mult)
             if k == 3:
                 nc.vector.tensor_tensor(den[t][:], den[t][:], rho_t[t][:], ALU.mult)
             if k == 4:
-                nc.vector.tensor_tensor(num[:, t, :], num[:, t, :], por_t[t][:], ALU.add)
+                nc.vector.tensor_tensor(num[:, t, cols], num[:, t, cols], por_t[t][:, cols], ALU.add)
             if k == 5:
-                parts = 2 if t == PACK - 1 else 1
-                for h in range(parts):
-                    cols = slice(h * U // parts, (h + 1) * U // parts)
-                    nc.vector.tensor_tensor(num[:, t, cols], num[:, t, cols], den[t][:, cols], ALU.mult)
-                    nc.scalar.activation(num[:, t, cols], num[:, t, cols], ACT.Ln, scale=LN_SCALE)
+                nc.vector.tensor_tensor(num[:, t, cols], num[:, t, cols], den[t][:, cols], ALU.mult)
+                nc.scalar.activation(num[:, t, cols], num[:, t, cols], ACT.Ln, scale=LN_SCALE)
 
-        for t in range(PACK):
-            fetch(t)
-        for t in range(PACK):
-            for k in range(6):
-                step(t, k)
+        def log_den(ts):
+            for t in ts:
+                nc.scalar.activation(big[:, t, :], por_t[t][:], ACT.Square)
+            for t in ts:
+                nc.scalar.activation(big[:, t, :], big[:, t, :], ACT.Ln, scale=LN_SCALE)
 
-        chunks = U // CHUNK
-        refl = [keep.tile([P, CHUNK, PACK], F32, name=f"refl{c}") for c in range(chunks)]
-        hid = [keep.tile([P, CHUNK, PACK], BF16, name=f"hid{c}", align_bytes=64) for c in range(chunks)]
-        hq_w = [keep.tile([P, CHUNK], U32, name=f"hq_w{c}", align_bytes=64) for c in range(chunks)]
-        hq_s = [keep.tile([P, CHUNK], U8, name=f"hq_s{c}", align_bytes=64) for c in range(chunks)]
-        res = [keep.tile([P, CHUNK], F32, name=f"res{c}") for c in range(chunks)]
+        shift(0)
+        pore_term(den[0][:], 0, whole)
+        for t in range(1, SHIFT_ON_VECTOR):
+            shift(t)
+        pore_term(den[1][:], 1, whole)
+        pore_term(den[2][:, halves[0]], 2, halves[0])
+        rock_table(0)
+        rock_table(1)
+        late = keep.tile([P, U // 2], F32, name="late", tag="soft0")
+        pore_term(late[:], 2, halves[1])
+        for cols in halves:
+            fetch(0, cols)
+        fetch(1, whole)
+        square(0)
+        step(0, 0, halves[0])
+        rock_table(2)
+        step(0, 0, halves[1])
+        step(0, 1, halves[0])
+        rock_table(3)
+        step(0, 1, halves[1])
+        fetch(2, whole)
+        square(1)
+        gathered = keep.tile([P, U], F32)
+        nc.scalar.activation(gathered[:], fluid[3][:].indirect(fl_t[:]), ACT.Copy, bias=-0.3)
+        fetch(3, whole)
+        square(2)
+        square(3)
+        for cols in halves:
+            step(0, 2, cols)
+        for t, k in ((1, 0), (0, 3), (1, 1), (0, 4), (1, 2), (0, 5), (1, 3)):
+            step(t, k)
+        log_den((0, 1))
+        den.append(keep.tile([P, U], F32, name="den3", tag="den0"))
+        step(2, 0, halves[0])
+        step(1, 4)
+        step(2, 0, halves[1], late[:])
+        step(1, 5)
+        nc.vector.tensor_tensor(den[3][:], gathered[:], por_t[3][:], ALU.mult)
+        for t, k in ((2, 1), (3, 0), (2, 2), (3, 1), (2, 3), (3, 2), (2, 4), (3, 3), (2, 5)):
+            step(t, k)
+            if (t, k) == (3, 2):
+                log_den((2, 3))
+        for k in (4, 5):
+            for cols in halves:
+                step(3, k, cols)
+        for cols in halves:
+            for ts in (slice(0, 2), slice(2, 4)):
+                nc.vector.tensor_tensor(num[:, ts, cols], num[:, ts, cols], big[:, ts, cols], ALU.subtract)
+
+        starts = [sum(WIDTHS[:c]) for c in range(len(WIDTHS))]
+        spans = [slice(a, a + w) for a, w in zip(starts, WIDTHS)]
+        hid = []
 
         def weigh(c):
-            cols = slice(c * CHUNK, (c + 1) * CHUNK)
-            nc.scalar.activation(refl[c][:], num[:, :, cols].rearrange("p t c -> p c t"), ACT.Tanh, scale=0.25)
-            nc.vector.tensor_tensor(
-                hid[c][:], refl[c][:], unit_t[:].unsqueeze(1).to_broadcast([P, CHUNK, PACK]), ALU.mult
-            )
+            refl = keep.tile([P, WIDTHS[c], PACK], F32, name=f"refl{c}")
+            hid.append(keep.tile([P, WIDTHS[c], PACK], BF16, name=f"hid{c}", align_bytes=64))
+            nc.scalar.activation(refl[:], num[:, :, spans[c]].rearrange("p t c -> p c t"), ACT.Tanh, scale=0.25)
+            nc.vector.tensor_tensor(hid[c][:], refl[:], unit_rep[:, 0 : WIDTHS[c], :], ALU.mult)
 
         def finish(c):
-            cols = slice(c * CHUNK, (c + 1) * CHUNK)
-            nc.vector.quantize_mx(
-                out=hq_w[c][:].bitcast(FP8X4), scales=hq_s[c][:], in_=hid[c][:].rearrange("p c t -> p (c t)")
-            )
-            acc = psum.tile([P, S], F32, name=f"bank0{c}")
+            hq_w = keep.tile([P, WIDTHS[c]], U32, name=f"hq_w{c}", align_bytes=64)
+            hq_s = keep.tile([P, WIDTHS[c]], U8, name=f"hq_s{c}", align_bytes=64)
+            res = keep.tile([P, WIDTHS[c]], F32, name=f"res{c}")
+            nc.vector.quantize_mx(out=hq_w[:].bitcast(FP8X4), scales=hq_s[:], in_=hid[c][:].rearrange("p c t -> p (c t)"))
+            acc = psum.tile([P, S], F32, name=f"bank0{c % PACK}")
             nc.tensor.matmul_mx(
-                out=acc[:, 0:CHUNK],
+                out=acc[:, 0 : WIDTHS[c]],
                 lhsT=w3_w[:].bitcast(FP4X4),
                 lhsT_scale=w3_s[:],
-                rhs=hq_w[c][:].bitcast(FP8X4),
-                rhs_scale=hq_s[c][:],
+                rhs=hq_w[:].bitcast(FP8X4),
+                rhs_scale=hq_s[:],
                 start=True,
                 stop=True,
             )
-            nc.scalar.copy(res[c][:], acc[:, 0:CHUNK])
-            nc.sync.dma_start(out=out[:, cols], in_=res[c][:])
+            nc.scalar.copy(res[:], acc[:, 0 : WIDTHS[c]])
+            nc.sync.dma_start(out=out[:, spans[c]], in_=res[:])
 
-        for c in range(chunks):
-            cols = slice(c * CHUNK, (c + 1) * CHUNK)
-            nc.vector.tensor_tensor(num[:, :, cols], num[:, :, cols], big[:, :, cols], ALU.subtract)
         weigh(0)
-        for c in range(1, chunks):
+        for c in range(1, len(WIDTHS)):
             weigh(c)
             finish(c - 1)
-        finish(chunks - 1)
+        finish(len(WIDTHS) - 1)

from contextlib import ExitStack

import concourse.mybir as mybir

K, T, S, N, H, U = 512, 1024, 512, 128, 512, 1024
FLOPS = 2 * (2 * K * H * S + H * N * U)

F32 = mybir.dt.float32
BF16 = mybir.dt.bfloat16
I32 = mybir.dt.int32
U32 = mybir.dt.uint32
U16 = mybir.dt.uint16
U8 = mybir.dt.uint8
FP8X4 = mybir.dt.float8_e4m3fn_x4
FP4X4 = mybir.dt.float4_e2m1fn_x4
ALU = mybir.AluOpType
ACT = mybir.ActivationFunctionType

P = 128
PACK = 4
CHUNK = 256
HALF = S // 2
WIDTHS = (256, 256, 256, 128, 128)
TINY = 1e-18
LN_SCALE = 2.0**-16
SHIFT_ON_VECTOR = 3
POR_SLOT = (2, 0, 8, 10)
RHO_SLOT = (1, 9, 6, 12)


def load_scale_rows(queue, plane, rows, quadrants=range(4)):
    for q in quadrants:
        queue.dma_start(out=plane[32 * q : 32 * q + 4, :].bitcast(I32), in_=rows[4 * q : 4 * q + 4, :].bitcast(I32))


def tile_picked_ygassm_refl_p_kernel(
    tc, x_words, x_scales, w1_words, w1_scales, w2_words, w2_scales, por, rho, unit, w3_words, w3_scales, offs, rk, fl, out
):
    nc = tc.nc
    with ExitStack() as ctx:
        keep = ctx.enter_context(tc.tile_pool(name="keep", bufs=1))
        psum = ctx.enter_context(tc.psum_pool(name="psum", bufs=1))

        offs_t = keep.tile([P, S // 16], U16)
        rk_t = keep.tile([P, U // 16], U16)
        fl_t = keep.tile([P, U // 16], U16)
        x_w = keep.tile([P, T], U32, align_bytes=64, tag="in0")
        x_s = keep.tile([P, T], U8, align_bytes=64, tag="in1")

        xg_w = []
        xg_s = []

        def load_words(words):
            w_raw = keep.tile([P, 2 * H], U8, name="w_raw", align_bytes=64, tag="in2")
            nc.sync.dma_start(out=w_raw[:].bitcast(I32), in_=words[0].bitcast(I32))
            return w_raw

        def load_scales(scales, tag):
            s_raw = keep.tile([P, H], U8, name="s_raw", align_bytes=64, tag=tag)
            nc.gpsimd.memset(s_raw[:].bitcast(I32), 0)
            load_scale_rows(nc.sync, s_raw, scales[0])
            return s_raw

        def deal_words(w_raw, tag):
            w_deal = keep.tile([P, 2 * H], U8, name="w_deal", align_bytes=64, tag=tag)
            nc.vector.tensor_copy(
                out=w_deal[:].rearrange("p (t m b) -> p t m b", t=PACK, b=2),
                in_=w_raw[:].rearrange("p (m t b) -> p t m b", t=PACK, b=2),
            )
            return w_deal

        def deal_scales(s_raw, tag):
            s_deal = keep.tile([P, H], U8, name="s_deal", align_bytes=64, tag=tag)
            nc.vector.tensor_copy(
                out=s_deal[:].rearrange("p (t m) -> p t m", t=PACK),
                in_=s_raw[:].rearrange("p (m t) -> p t m", t=PACK),
            )
            return s_deal

        def product(acc, w_deal, s_deal, t, h):
            nc.tensor.matmul_mx(
                out=acc,
                lhsT=w_deal[:, 2 * P * t : 2 * P * (t + 1)].bitcast(FP4X4),
                lhsT_scale=s_deal[:, P * t : P * (t + 1)],
                rhs=xg_w[h][:].bitcast(FP8X4),
                rhs_scale=xg_s[h][:],
                start=True,
                stop=True,
            )

        def pick(h, word_tag, scale_tag):
            entries = offs_t[:, h * HALF // 16 : (h + 1) * HALF // 16]
            xg_w.append(keep.tile([P, HALF], U32, name="xg_w", align_bytes=64, tag=word_tag))
            xg_s.append(keep.tile([P, HALF], U8, name="xg_s", align_bytes=64, tag=scale_tag))
            nc.vector.tensor_copy(out=xg_w[h][:], in_=x_w[:].indirect(entries))
            nc.vector.tensor_copy(out=xg_s[h][:], in_=x_s[:].indirect(entries))

        def load_planes(src, name, slots):
            rows = src.rearrange("(p t) r -> p t r", t=PACK)
            tiles = [keep.tile([P, U], F32, name=f"{name}{t}", align_bytes=64, tag=f"in{slots[t]}") for t in range(PACK)]
            for t in range(PACK):
                nc.sync.dma_start(out=tiles[t][:], in_=rows[:, t, :])
            return tiles

        nc.vector.memset(x_s[:].bitcast(I32), 0)
        nc.sync.dma_start(out=offs_t[:], in_=offs)
        nc.sync.dma_start(out=fl_t[:], in_=fl)
        nc.sync.dma_start(out=rk_t[:], in_=rk)
        w2_raw = load_words(w2_words)
        load_scale_rows(nc.sync, x_s, x_scales[0], range(0, 1))
        nc.sync.dma_start(out=x_w[:].bitcast(I32), in_=x_words[0].rearrange("p n t -> p (n t)").bitcast(I32))
        load_scale_rows(nc.sync, x_s, x_scales[0], range(1, 4))
        s2_raw = load_scales(w2_scales, "in3")
        w2_deal = deal_words(w2_raw, "in8")
        pick(0, "in6", "in7")
        s2_deal = deal_scales(s2_raw, "in10")
        pick(1, "in12", "in3")
        fluid_bank = [psum.tile([P, S], F32, name=f"bank0{b}") for b in range(PACK)]
        for h in range(2):
            for t in range(PACK):
                acc = fluid_bank[2 * h + t // 2][:, (t % 2) * HALF : (t % 2 + 1) * HALF]
                product(acc, w2_deal, s2_deal, t, h)
        w1_deal = deal_words(load_words(w1_words), "in9")
        s1_raw = load_scales(w1_scales, "in1")

        unit_t = keep.tile([P, PACK], F32, align_bytes=64, tag="in0")
        nc.sync.dma_start(out=unit_t[:], in_=unit.rearrange("(p t) o -> p (t o)", t=PACK))
        unit_rep = keep.tile([P, CHUNK, PACK], F32)
        nc.vector.tensor_copy(out=unit_rep[:], in_=unit_t[:].unsqueeze(1).to_broadcast([P, CHUNK, PACK]))
        por_t = load_planes(por, "por", POR_SLOT)

        fluid = [keep.tile([P, 3 * S], F32, name=f"fluid{t}") for t in range(PACK)]
        rock = [keep.tile([P, 3 * S], F32, name=f"rock{t}") for t in range(PACK)]
        slot0, slot1, slot2 = slice(0, S), slice(S, 2 * S), slice(2 * S, 3 * S)
        last = keep.tile([P, S], F32, align_bytes=64, tag="in11")
        sig = [last[:] if b == 1 else fluid[b][:, slot2] for b in range(PACK)]
        plus_f = keep.tile([P, 2, PACK, HALF], F32)
        for b in range(PACK):
            nc.scalar.activation(sig[b], fluid_bank[b][:], ACT.Sigmoid, scale=-1.0)
        for b in (0, 2, 1, 3):
            nc.scalar.activation(sig[b], sig[b], ACT.Ln, bias=TINY)
            both = plus_f[:, b // 2, 2 * (b % 2) : 2 * (b % 2) + 2, :].rearrange("p t c -> p (t c)")
            nc.vector.scalar_tensor_tensor(both, sig[b], -1.0, fluid_bank[b][:], ALU.mult, ALU.max)
        s1_deal = deal_scales(s1_raw, "in11")
        rock_bank = [psum.tile([P, S], F32, name=f"bank1{t}") for t in range(PACK)]
        for t in range(PACK):
            for h in range(2):
                product(rock_bank[t][:, h * HALF : (h + 1) * HALF], w1_deal, s1_deal, t, h)
        for t in range(PACK):
            nc.vector.tensor_scalar(rock[t][:, slot2], rock_bank[t][:], 40.0, None, ALU.min)

        rho_t = load_planes(rho, "rho", RHO_SLOT)
        w3_w = keep.tile([P, 2 * N], U8, align_bytes=64, tag="in7")
        w3_s = keep.tile([P, N], U8, align_bytes=64)
        nc.sync.dma_start(out=w3_w[:].bitcast(I32), in_=w3_words[0].bitcast(I32))
        nc.gpsimd.memset(w3_s[:].bitcast(I32), 0)
        load_scale_rows(nc.sync, w3_s, w3_scales[0])

        for t in range(PACK):
            both = fluid[t][:, slot1].rearrange("p (h c) -> p h c", h=2)
            nc.scalar.activation(both, plus_f[:, :, t, :], ACT.Ln, scale=0.5, bias=0.1)
        for t in range(PACK):
            nc.scalar.activation(fluid[t][:, slot0 if t == PACK - 1 else slot2], fluid[t][:, slot1], ACT.Exp, scale=-1.0)
        for t in range(PACK):
            nc.scalar.activation(rock[t][:, slot1], rock[t][:, slot2], ACT.Exp)
        soft = [keep.tile([P, S], F32, name=f"soft{t}") for t in range(PACK)]
        for t in range(PACK):
            nc.scalar.activation(soft[t][:], rock[t][:, slot1], ACT.Ln, bias=1.0)

        big = keep.tile([P, PACK, U], F32)
        num = keep.tile([P, PACK, U], F32)
        den = [keep.tile([P, U], F32, name=f"den{t}") for t in range(PACK - 1)]
        whole = slice(0, U)
        halves = (slice(0, U // 2), slice(U // 2, U))

        def entries(tile, cols):
            return tile[:, cols.start // 16 : cols.stop // 16]

        def shift(t):
            nc.vector.tensor_scalar(fluid[t][:, slot0], fluid[t][:, slot2], -0.3, None, ALU.add)

        def pore_term(dst, t, cols):
            nc.vector.tensor_tensor(dst, fluid[t][:].indirect(entries(fl_t, cols)), por_t[t][:, cols], ALU.mult)

        def rock_table(t):
            nc.vector.tensor_tensor(rock[t][:, slot0], soft[t][:], rock_bank[t][:], ALU.max)

        def fetch(t, cols):
            nc.scalar.activation(big[:, t, cols], rock[t][:].indirect(entries(rk_t, cols)), ACT.Copy, bias=1.9)

        def square(t):
            nc.scalar.activation(num[:, t, :], big[:, t, :], ACT.Square, scale=0.2, bias=1.2)

        def step(t, k, cols=whole, src=None):
            if k == 0:
                src = den[t][:, cols] if src is None else src
                nc.vector.scalar_tensor_tensor(den[t][:, cols], src, 0.06, big[:, t, cols], ALU.add, ALU.mult)
            if k == 1:
                nc.vector.scalar_tensor_tensor(den[t][:, cols], den[t][:, cols], 0.36, big[:, t, cols], ALU.add, ALU.mult)
            if k == 2:
                nc.vector.scalar_tensor_tensor(por_t[t][:, cols], big[:, t, cols], -1.5, den[t][:, cols], ALU.add, ALU.mult)
            if k == 3:
                nc.vector.tensor_tensor(den[t][:], den[t][:], rho_t[t][:], ALU.mult)
            if k == 4:
                nc.vector.tensor_tensor(num[:, t, cols], num[:, t, cols], por_t[t][:, cols], ALU.add)
            if k == 5:
                nc.vector.tensor_tensor(num[:, t, cols], num[:, t, cols], den[t][:, cols], ALU.mult)
                nc.scalar.activation(num[:, t, cols], num[:, t, cols], ACT.Ln, scale=LN_SCALE)

        def log_den(ts):
            for t in ts:
                nc.scalar.activation(big[:, t, :], por_t[t][:], ACT.Square)
            for t in ts:
                nc.scalar.activation(big[:, t, :], big[:, t, :], ACT.Ln, scale=LN_SCALE)

        shift(0)
        pore_term(den[0][:], 0, whole)
        for t in range(1, SHIFT_ON_VECTOR):
            shift(t)
        pore_term(den[1][:], 1, whole)
        pore_term(den[2][:, halves[0]], 2, halves[0])
        rock_table(0)
        rock_table(1)
        late = keep.tile([P, U // 2], F32, name="late", tag="soft0")
        pore_term(late[:], 2, halves[1])
        for cols in halves:
            fetch(0, cols)
        fetch(1, whole)
        square(0)
        step(0, 0, halves[0])
        rock_table(2)
        step(0, 0, halves[1])
        step(0, 1, halves[0])
        rock_table(3)
        step(0, 1, halves[1])
        fetch(2, whole)
        square(1)
        gathered = keep.tile([P, U], F32)
        nc.scalar.activation(gathered[:], fluid[3][:].indirect(fl_t[:]), ACT.Copy, bias=-0.3)
        fetch(3, whole)
        square(2)
        square(3)
        for cols in halves:
            step(0, 2, cols)
        for t, k in ((1, 0), (0, 3), (1, 1), (0, 4), (1, 2), (0, 5), (1, 3)):
            step(t, k)
        log_den((0, 1))
        den.append(keep.tile([P, U], F32, name="den3", tag="den0"))
        step(2, 0, halves[0])
        step(1, 4)
        step(2, 0, halves[1], late[:])
        step(1, 5)
        nc.vector.tensor_tensor(den[3][:], gathered[:], por_t[3][:], ALU.mult)
        for t, k in ((2, 1), (3, 0), (2, 2), (3, 1), (2, 3), (3, 2), (2, 4), (3, 3), (2, 5)):
            step(t, k)
            if (t, k) == (3, 2):
                log_den((2, 3))
        for k in (4, 5):
            for cols in halves:
                step(3, k, cols)
        for cols in halves:
            for ts in (slice(0, 2), slice(2, 4)):
                nc.vector.tensor_tensor(num[:, ts, cols], num[:, ts, cols], big[:, ts, cols], ALU.subtract)

        starts = [sum(WIDTHS[:c]) for c in range(len(WIDTHS))]
        spans = [slice(a, a + w) for a, w in zip(starts, WIDTHS)]
        hid = []

        def weigh(c):
            refl = keep.tile([P, WIDTHS[c], PACK], F32, name=f"refl{c}")
            hid.append(keep.tile([P, WIDTHS[c], PACK], BF16, name=f"hid{c}", align_bytes=64))
            nc.scalar.activation(refl[:], num[:, :, spans[c]].rearrange("p t c -> p c t"), ACT.Tanh, scale=0.25)
            nc.vector.tensor_tensor(hid[c][:], refl[:], unit_rep[:, 0 : WIDTHS[c], :], ALU.mult)

        def finish(c):
            hq_w = keep.tile([P, WIDTHS[c]], U32, name=f"hq_w{c}", align_bytes=64)
            hq_s = keep.tile([P, WIDTHS[c]], U8, name=f"hq_s{c}", align_bytes=64)
            res = keep.tile([P, WIDTHS[c]], F32, name=f"res{c}")
            nc.vector.quantize_mx(out=hq_w[:].bitcast(FP8X4), scales=hq_s[:], in_=hid[c][:].rearrange("p c t -> p (c t)"))
            acc = psum.tile([P, S], F32, name=f"bank0{c % PACK}")
            nc.tensor.matmul_mx(
                out=acc[:, 0 : WIDTHS[c]],
                lhsT=w3_w[:].bitcast(FP4X4),
                lhsT_scale=w3_s[:],
                rhs=hq_w[:].bitcast(FP8X4),
                rhs_scale=hq_s[:],
                start=True,
                stop=True,
            )
            nc.scalar.copy(res[:], acc[:, 0 : WIDTHS[c]])
            nc.sync.dma_start(out=out[:, spans[c]], in_=res[:])

        weigh(0)
        for c in range(1, len(WIDTHS)):
            weigh(c)
            finish(c - 1)
        finish(len(WIDTHS) - 1)
